import numpy as np
import ml_dtypes


def mxq(x, axis, fmt="e4m3"):
    dtype, down = {"e4m3": (ml_dtypes.float8_e4m3fn, 7), "e5m2": (ml_dtypes.float8_e5m2, 14)}[fmt]
    v = np.moveaxis(np.asarray(x, np.float32).astype(ml_dtypes.bfloat16).astype(np.float64), axis, -1)
    blocks = v.reshape(v.shape[:-1] + (-1, 32))
    amax = np.abs(blocks).max(-1, keepdims=True)
    byte = np.maximum(np.where(amax > 0, np.frexp(amax)[1] - 1 + 127, 0) - down, 1)
    scale = np.exp2(byte - 127.0)
    codes = (blocks / scale).astype(np.float32).astype(dtype).astype(np.float64)
    return np.moveaxis((codes * scale).reshape(v.shape), -1, axis)


WIDE = False


def mx_kscale(k):
    if not WIDE:
        return np.ones(k)
    levels = np.array([10, -10, 5, -5, 0])
    if k % 512:
        return np.exp2(np.random.permutation(np.resize(levels, k // 32))).repeat(32)
    a = np.empty((k // 512, 16))
    for p in range(k // 512):
        a[p, :8] = np.random.permutation(np.resize(levels, 8))
        for g in range(8):
            far = levels[np.abs(levels - a[p, g]) >= 10]
            a[p, g + 8] = far[np.random.randint(len(far))]
    return np.exp2(a.ravel()).repeat(32)


def f64(x):
    return np.asarray(x).astype(np.float64)


def striped(idx):
    return np.tile(np.asarray(idx).reshape(-1, 16).T, (8, 1)).astype(np.uint16)


def unstriped(offs):
    return offs[:16].T.reshape(-1).astype(np.int64)


E2M1 = np.array([0.0, 0.5, 1.0, 1.5, 2.0, 3.0, 4.0, 6.0, -0.0, -0.5, -1.0, -1.5, -2.0, -3.0, -4.0, -6.0])


def pack_weight(w, fmt):
    k, n = w.shape
    w = f64(np.asarray(w, np.float32).astype(ml_dtypes.bfloat16)).reshape(k // 32, 32, n)
    amax = np.abs(w).max(1)
    if fmt == "e4m3":
        byte = np.frexp(amax)[1] - 1 + 127 - 7
    else:
        mant, ex = np.frexp(amax / 6.0)
        byte = np.where(mant > 0.5, ex, ex - 1) + 127
    byte = np.clip(np.where(amax > 0, byte, 1), 1, 254)
    scaled = (w * np.exp2(127.0 - byte)[:, None, :]).reshape(k, n).astype(np.float32)
    by_word = np.ascontiguousarray(scaled.reshape(k // 512, 128, 4, n).transpose(0, 1, 3, 2))
    if fmt == "e4m3":
        words = by_word.astype(ml_dtypes.float8_e4m3fn).view(np.uint8)
    else:
        c = by_word.astype(ml_dtypes.float4_e2m1fn).view(np.uint8) & 0xF
        words = (c[..., 0::2] | (c[..., 1::2] << 4)).reshape(k // 512, 128, 2 * n)
    return np.ascontiguousarray(words), np.ascontiguousarray(byte.astype(np.uint8).reshape(k // 512, 16, n))


def unpack_weight(words, scales, fmt):
    g, _, n = scales.shape
    words = np.ascontiguousarray(words).reshape(g, 128, n, -1)
    if fmt == "e4m3":
        vals = words.view(ml_dtypes.float8_e4m3fn).astype(np.float64)
    else:
        nib = np.empty((g, 128, n, 4), np.uint8)
        nib[..., 0::2] = words & 0xF
        nib[..., 1::2] = words >> 4
        vals = E2M1[nib]
    vals = vals * np.repeat(np.exp2(scales.astype(np.float64) - 127.0), 8, axis=1)[..., None]
    return vals.transpose(0, 1, 3, 2).reshape(g * 512, n)


D, E, T, I, Q = 512, 512, 1024, 256, 512


def setup_inputs():
    n = np.random.standard_normal
    idx = np.random.permutation(T)[:I]
    fd = mx_kscale(D)
    fq = mx_kscale(Q)
    keysp = pack_weight(n((D, T)) / fd[:, None], "e2m1")
    return {
        "query": (n((D, Q)) * 0.7 / np.sqrt(D) * fd[:, None]).astype(np.float32),
        "keys_words": keysp[0],
        "keys_scales": keysp[1],
        "qs": (np.random.uniform(0.1, 0.4, (Q, 1)) * fq[:, None]).astype(np.float32),
        "grows": (n((Q, E)) / fq[:, None]).astype(np.float32),
        "old": (n((E, T)) * 2.0).astype(np.float32),
        "fade": (np.random.uniform(0.5, 1.0, (1, T))).astype(np.float32),
        "offs": striped(idx),
    }


def reference(query, keys_words, keys_scales, qs, grows, old, fade, offs):
    idx = unstriped(offs)
    keysu = unpack_weight(keys_words, keys_scales, "e2m1")
    queryq = mxq(f64(query), 0, "e4m3")
    keysidxg = keysu[:, idx]
    a = queryq.T @ keysidxg
    p = np.exp(a - np.max(a, axis=1, keepdims=True))
    n2 = np.sqrt(np.sum(np.square(p), axis=1, keepdims=True))
    w = p / n2
    wq = w * f64(qs)
    growsq = mxq(f64(grows), 0, "e4m3")
    wqq = mxq(wq, 0, "e4m3")
    gv = growsq.T @ wqq
    gf = np.zeros((E, T))
    gf[:, idx] = gv
    y = f64(old) * f64(fade) + gf
    return y

@@ -1,0 +1,180 @@
+from contextlib import ExitStack
+
+import concourse.mybir as mybir
+from concourse.masks import make_identity
+
+D, E, T, I, Q = 512, 512, 1024, 256, 512
+P = 128
+FLOPS = 2 * D * Q * I + 2 * Q * E * I
+
+F32 = mybir.dt.float32
+BF16 = mybir.dt.bfloat16
+I32 = mybir.dt.int32
+U32 = mybir.dt.uint32
+U16 = mybir.dt.uint16
+U8 = mybir.dt.uint8
+FP8X4 = mybir.dt.float8_e4m3fn_x4
+FP4X4 = mybir.dt.float4_e2m1fn_x4
+ALU = mybir.AluOpType
+ACT = mybir.ActivationFunctionType
+AX = mybir.AxisListType
+
+
+def tile_attend_bunitweights_v_kernel(tc, query, keys_words, keys_scales, qs, grows, old, fade, offs, out):
+    nc = tc.nc
+    with ExitStack() as ctx:
+        sb = ctx.enter_context(tc.tile_pool(name="sb", bufs=1))
+        ps = ctx.enter_context(tc.psum_pool(name="ps", bufs=1))
+
+        def sbuf(name, shape, dtype, tag=None):
+            return sb.tile(shape, dtype, name=name, tag=tag or name, align_bytes=64)
+
+        def bank(b, name):
+            return ps.tile([P, 512], F32, name=name, tag="bank%d" % b)
+
+        offsets = sb.tile([P, I // 16], U16, name="offsets")
+        kwords = sbuf("kwords", [P, T], U16)
+        kscales = sbuf("kscales", [P, T], U8)
+        nc.vector.memset(kscales[:].bitcast(I32), 0)
+        nc.sync.dma_start(out=kwords[:].bitcast(I32), in_=keys_words[0].bitcast(I32))
+        nc.sync.dma_start(offsets[:], offs)
+        for g in range(4):
+            nc.scalar.dma_start(out=kscales[32 * g : 32 * g + 4, :].bitcast(I32), in_=keys_scales[0, 4 * g : 4 * g + 4, :].bitcast(I32))
+        qv = query.rearrange("(p j) q -> p j q", j=4)
+        qraw = [sbuf("qraw%d" % h, [P, 4, 256], F32) for h in range(2)]
+        for h in range(2):
+            nc.sync.dma_start(out=qraw[h][:], in_=qv[:, :, 256 * h : 256 * (h + 1)])
+        warm = sbuf("warm", [P, 1], F32)
+        half = sbuf("half", [P, 2], F32)
+        nc.vector.memset(half[:], -0.5)
+        nc.scalar.activation(warm[:], half[:, 0:1], ACT.Exp)
+        ident = sbuf("ident", [P, P], F32)
+        make_identity(nc, ident[:])
+        small = sbuf("small", [P, P + 4], F32)
+        nc.gpsimd.memset(small[:], 0.0)
+        nc.sync.dma_start(out=small[:, P : P + 4], in_=qs.rearrange("(p r) o -> p (r o)", r=4))
+        nc.sync.dma_start(out=small[0:8, 0:P], in_=fade.rearrange("o (c p) -> (o c) p", p=P))
+        graw = sbuf("graw", [P, 4, E], F32, tag="warm")
+        nc.sync.dma_start(out=graw[:], in_=grows.rearrange("(p j) e -> p j e", j=4))
+
+        kw = sbuf("kw", [P, I], U16)
+        ks = sbuf("ks", [P, I], U8)
+        nc.vector.tensor_copy(kw[:], kwords[:].indirect(offsets[:]))
+        nc.vector.tensor_copy(ks[:], kscales[:].indirect(offsets[:]))
+
+        qcodes = [sbuf("qcodes%d" % r, [P, P], U32) for r in range(4)]
+        qscale = [sbuf("qscale%d" % r, [P, P], U8) for r in range(4)]
+
+        def weave_query(engine_copy, h, r0, r1):
+            g = sbuf("qg%d_%d" % (h, r0), [P, r1 - r0, 64, 4], BF16)
+            src = qraw[h][:].rearrange("p j (m r) -> p m j r", r=4)[:, :, :, r0:r1]
+            engine_copy(g[:].rearrange("p r m j -> p m j r"), src)
+            return g
+
+        def quant_query(g, h, r0, r1):
+            for r in range(r0, r1):
+                nc.vector.quantize_mx(out=qcodes[r][:, 64 * h : 64 * (h + 1)].bitcast(FP8X4), scales=qscale[r][:, 64 * h : 64 * (h + 1)],
+                                      in_=g[:, r - r0, :, :].rearrange("p m j -> p (m j)"))
+
+        g0 = weave_query(nc.vector.tensor_copy, 0, 0, 4)
+        quant_query(g0, 0, 0, 4)
+        g1a = weave_query(nc.vector.tensor_copy, 1, 0, 2)
+        g1b = weave_query(nc.scalar.copy, 1, 2, 4)
+        quant_query(g1a, 1, 0, 2)
+        quant_query(g1b, 1, 2, 4)
+
+        ov = old.rearrange("(k p) t -> p k t", p=P)
+        oraw = [sbuf("oraw%d" % u, [P, 4, 256], F32, tag=("kwords", "kscales", "qraw0", "qraw1")[u]) for u in range(4)]
+        for u in range(4):
+            nc.sync.dma_start(out=oraw[u][:], in_=ov[:, :, 256 * u : 256 * (u + 1)])
+
+        scores = [bank(r, "scores%d" % r) for r in range(4)]
+        for r in range(4):
+            nc.tensor.matmul_mx(out=scores[r][:, 0:I], lhsT=qcodes[r][:].bitcast(FP8X4), lhsT_scale=qscale[r][:],
+                                rhs=kw[:].bitcast(FP4X4), rhs_scale=ks[:], start=True, stop=True)
+        neg2 = [sbuf("neg2_%d" % r, [P, I], F32) for r in range(4)]
+        neg2max = sbuf("neg2max", [P, 4], F32)
+        negmax = sbuf("negmax", [P, 4], F32)
+        pexp = [sbuf("pexp%d" % r, [P, I], F32) for r in range(4)]
+        psq = [sbuf("psq%d" % r, [P, I], F32) for r in range(4)]
+        ssum = [sbuf("ssum%d" % h, [P, 2], F32) for h in range(2)]
+        rs = [sbuf("rs%d" % h, [P, 2], F32) for h in range(2)]
+        wq = sbuf("wq", [P, 4, I], BF16)
+        for r in range(4):
+            nc.vector.tensor_scalar(neg2[r][:], scores[r][:, 0:I], -2.0, None, ALU.mult, ALU.min, accum_out=neg2max[:, r : r + 1])
+        nc.vector.tensor_scalar(negmax[:], neg2max[:], 0.5, None, ALU.mult)
+        for r in range(4):
+            nc.scalar.activation(psq[r][:], neg2[r][:], ACT.Exp, bias=neg2max[:, r : r + 1], scale=-1.0, accum_out=ssum[r // 2][:, r % 2 : r % 2 + 1])
+            if r % 2:
+                nc.gpsimd.tensor_tensor(rs[r // 2][:], ssum[r // 2][:], half[:], ALU.pow)
+        for r in range(4):
+            nc.scalar.activation(pexp[r][:], neg2[r][:], ACT.Exp, bias=negmax[:, r : r + 1], scale=-0.5)
+
+        fcols = sbuf("fcols", [P, 8], F32)
+        fb = bank(3, "fbank")
+        nc.tensor.transpose(fb[:, 0:P], small[:, 0:P], ident[:])
+        nc.scalar.copy(fcols[:], fb[:, 0:8])
+
+        gcodes = [sbuf("gcodes%d" % h, [P, 256], U32) for h in range(2)]
+        gscale = [sbuf("gscale%d" % h, [P, 256], U8) for h in range(2)]
+        gg = [sbuf("gg%d" % h, [P, 256, 4], BF16) for h in range(2)]
+
+        def weave_grows(engine_copy, h):
+            src = graw[:, :, 256 * h : 256 * (h + 1)].rearrange("p j (c i) -> p c j i", i=4)
+            engine_copy(gg[h][:].rearrange("p (c i) j -> p c j i", i=4), src)
+
+        def quant_grows(h):
+            nc.vector.quantize_mx(out=gcodes[h][:].bitcast(FP8X4), scales=gscale[h][:], in_=gg[h][:].rearrange("p e j -> p (e j)"))
+
+        weave_grows(nc.vector.tensor_copy, 0)
+        weave_grows(nc.scalar.copy, 1)
+        for r in range(4):
+            nc.vector.tensor_scalar(wq[:, r, :], pexp[r][:], rs[r // 2][:, r % 2 : r % 2 + 1], small[:, P + r : P + r + 1], ALU.mult, ALU.mult)
+        quant_grows(0)
+        wg = sbuf("wg", [P, I, 4], BF16)
+        nc.vector.tensor_copy(wg[:].rearrange("p (c i) r -> p c r i", i=4), wq[:].rearrange("p r (c i) -> p c r i", i=4))
+        quant_grows(1)
+        wcodes = sbuf("wcodes", [P, I], U32)
+        wscale = sbuf("wscale", [P, I], U8)
+        nc.vector.quantize_mx(out=wcodes[:].bitcast(FP8X4), scales=wscale[:], in_=wg[:].rearrange("p i r -> p (i r)"))
+
+        gv = [sbuf("gv%d" % k, [P, I], F32) for k in range(4)]
+        for k in range(4):
+            acc = bank(k, "gvacc%d" % k)
+            cols = slice(P * (k % 2), P * (k % 2 + 1))
+            nc.tensor.matmul_mx(out=acc[:, 0:I], lhsT=gcodes[k // 2][:, cols].bitcast(FP8X4), lhsT_scale=gscale[k // 2][:, cols],
+                                rhs=wcodes[:].bitcast(FP8X4), rhs_scale=wscale[:], start=True, stop=True)
+            nc.scalar.copy(gv[k][:], acc[:, 0:I])
+
+        faded = [sbuf("faded%d" % c, [P, E], F32) for c in range(8)]
+        for c in range(8):
+            fw = bank((4, 5, 4, 5, 0, 1, 0, 1)[c], "fw%d" % c)
+            for k in range(4):
+                nc.tensor.transpose(fw[:, P * k : P * (k + 1)], oraw[c // 2][:, k, P * (c % 2) : P * (c % 2 + 1)], ident[:])
+            nc.scalar.activation(faded[c][:], fw[:], ACT.Copy, scale=fcols[:, c : c + 1])
+
+        window = [sbuf("window%d" % k, [P, T], F32) for k in range(4)]
+        for k in range(4):
+            nc.vector.memset(window[k][:], 0.0)
+
+        def scatter(k):
+            nc.vector.tensor_copy(window[k][:].indirect(offsets[:]), gv[k][:])
+
+        def finish(k):
+            for h in range(2):
+                n = 2 * k + h
+                bk = bank((6, 7, 4, 5, 2, 3, 6, 7)[n], "back%d" % n)
+                for c in range(4):
+                    nc.tensor.transpose(bk[:, P * c : P * (c + 1)], faded[4 * h + c][:, P * k : P * (k + 1)], ident[:])
+                res = sbuf("res%d" % n, [P, 512], F32)
+                nc.vector.tensor_tensor(res[:], bk[:], window[k][:, 512 * h : 512 * (h + 1)], ALU.add)
+                nc.sync.dma_start(out=out[P * k : P * (k + 1), 512 * h : 512 * (h + 1)], in_=res[:])
+
+        scatter(0)
+        scatter(1)
+        finish(0)
+        scatter(2)
+        finish(1)
+        scatter(3)
+        finish(2)
+        finish(3)

@@ -39,7 +39,7 @@ def tile_attend_bunitweights_v_kernel(tc, query, keys_words, keys_scales, qs, gr
         nc.sync.dma_start(out=kwords[:].bitcast(I32), in_=keys_words[0].bitcast(I32))
         nc.sync.dma_start(offsets[:], offs)
         for g in range(4):
-            nc.scalar.dma_start(out=kscales[32 * g : 32 * g + 4, :].bitcast(I32), in_=keys_scales[0, 4 * g : 4 * g + 4, :].bitcast(I32))
+            nc.sync.dma_start(out=kscales[32 * g : 32 * g + 4, :].bitcast(I32), in_=keys_scales[0, 4 * g : 4 * g + 4, :].bitcast(I32))
         qv = query.rearrange("(p j) q -> p j q", j=4)
         qraw = [sbuf("qraw%d" % h, [P, 4, 256], F32) for h in range(2)]
         for h in range(2):
@@ -48,20 +48,25 @@ def tile_attend_bunitweights_v_kernel(tc, query, keys_words, keys_scales, qs, gr
         half = sbuf("half", [P, 2], F32)
         nc.vector.memset(half[:], -0.5)
         nc.scalar.activation(warm[:], half[:, 0:1], ACT.Exp)
-        ident = sbuf("ident", [P, P], F32)
-        make_identity(nc, ident[:])
         small = sbuf("small", [P, P + 4], F32)
-        nc.gpsimd.memset(small[:], 0.0)
+        nc.vector.memset(small[:], 0.0)
+        window = [sbuf("window%d" % k, [P, T], F32) for k in range(3)]
+        for w in window:
+            nc.vector.memset(w[:], 0.0)
         nc.sync.dma_start(out=small[:, P : P + 4], in_=qs.rearrange("(p r) o -> p (r o)", r=4))
         nc.sync.dma_start(out=small[0:8, 0:P], in_=fade.rearrange("o (c p) -> (o c) p", p=P))
-        graw = sbuf("graw", [P, 4, E], F32, tag="warm")
-        nc.sync.dma_start(out=graw[:], in_=grows.rearrange("(p j) e -> p j e", j=4))
 
         kw = sbuf("kw", [P, I], U16)
         ks = sbuf("ks", [P, I], U8)
         nc.vector.tensor_copy(kw[:], kwords[:].indirect(offsets[:]))
         nc.vector.tensor_copy(ks[:], kscales[:].indirect(offsets[:]))
 
+        graw = sbuf("graw", [P, 4, E], F32, tag="kwords")
+        nc.sync.dma_start(out=graw[:], in_=grows.rearrange("(p j) e -> p j e", j=4))
+
+        for j, src in enumerate((window[0], qraw[0][:, 0, :])):
+            early = sbuf("early%d" % j, [P, 1], F32)
+            nc.gpsimd.tensor_copy(early[:], src[:, 0:1])
         qcodes = [sbuf("qcodes%d" % r, [P, P], U32) for r in range(4)]
         qscale = [sbuf("qscale%d" % r, [P, P], U8) for r in range(4)]
 
@@ -83,10 +88,17 @@ def tile_attend_bunitweights_v_kernel(tc, query, keys_words, keys_scales, qs, gr
         quant_query(g1a, 1, 0, 2)
         quant_query(g1b, 1, 2, 4)
 
+        ident = sbuf("ident", [P, P], F32, tag="qg1_0")
+        make_identity(nc, ident[:])
+        window.append(sbuf("window3", [P, T], F32, tag="qg1_2"))
+        nc.gpsimd.memset(window[3][:], 0.0)
+
         ov = old.rearrange("(k p) t -> p k t", p=P)
-        oraw = [sbuf("oraw%d" % u, [P, 4, 256], F32, tag=("kwords", "kscales", "qraw0", "qraw1")[u]) for u in range(4)]
-        for u in range(4):
+        oraw = [sbuf("oraw%d" % u, [P, 4, 256], F32, tag=("qraw0", "qg0_0")[u]) for u in range(2)]
+        for u in range(2):
             nc.sync.dma_start(out=oraw[u][:], in_=ov[:, :, 256 * u : 256 * (u + 1)])
+        oright = sbuf("oright", [P, 4, 512], F32, tag="qraw1")
+        nc.sync.dma_start(out=oright[:], in_=ov[:, :, 512:1024])
 
         scores = [bank(r, "scores%d" % r) for r in range(4)]
         for r in range(4):
@@ -99,14 +111,31 @@ def tile_attend_bunitweights_v_kernel(tc, query, keys_words, keys_scales, qs, gr
         psq = [sbuf("psq%d" % r, [P, I], F32) for r in range(4)]
         ssum = [sbuf("ssum%d" % h, [P, 2], F32) for h in range(2)]
         rs = [sbuf("rs%d" % h, [P, 2], F32) for h in range(2)]
-        wq = sbuf("wq", [P, 4, I], BF16)
         for r in range(4):
             nc.vector.tensor_scalar(neg2[r][:], scores[r][:, 0:I], -2.0, None, ALU.mult, ALU.min, accum_out=neg2max[:, r : r + 1])
-        nc.vector.tensor_scalar(negmax[:], neg2max[:], 0.5, None, ALU.mult)
         for r in range(4):
             nc.scalar.activation(psq[r][:], neg2[r][:], ACT.Exp, bias=neg2max[:, r : r + 1], scale=-1.0, accum_out=ssum[r // 2][:, r % 2 : r % 2 + 1])
             if r % 2:
                 nc.gpsimd.tensor_tensor(rs[r // 2][:], ssum[r // 2][:], half[:], ALU.pow)
+        gcodes = {}
+        gscale = {}
+
+        def weave_grows(engine_copy, e0, e1):
+            g = sbuf("gg%d" % e0, [P, e1 - e0, 4], BF16)
+            src = graw[:, :, e0:e1].rearrange("p j (c i) -> p c j i", i=4)
+            engine_copy(g[:].rearrange("p (c i) j -> p c j i", i=4), src)
+            return g
+
+        def quant_grows(g, e0, e1, tag=None):
+            codes = sbuf("gcodes%d" % e0, [P, e1 - e0], U32, tag=tag)
+            scale = sbuf("gscale%d" % e0, [P, e1 - e0], U8)
+            nc.vector.quantize_mx(out=codes[:].bitcast(FP8X4), scales=scale[:], in_=g[:].rearrange("p e j -> p (e j)"))
+            for e in range(e0, e1, P):
+                gcodes[e // P] = codes[:, e - e0 : e - e0 + P]
+                gscale[e // P] = scale[:, e - e0 : e - e0 + P]
+
+        ga = weave_grows(nc.vector.tensor_copy, 0, 128)
+        nc.vector.tensor_scalar(negmax[:], neg2max[:], 0.5, None, ALU.mult)
         for r in range(4):
             nc.scalar.activation(pexp[r][:], neg2[r][:], ACT.Exp, bias=negmax[:, r : r + 1], scale=-0.5)
 
@@ -115,66 +144,79 @@ def tile_attend_bunitweights_v_kernel(tc, query, keys_words, keys_scales, qs, gr
         nc.tensor.transpose(fb[:, 0:P], small[:, 0:P], ident[:])
         nc.scalar.copy(fcols[:], fb[:, 0:8])
 
-        gcodes = [sbuf("gcodes%d" % h, [P, 256], U32) for h in range(2)]
-        gscale = [sbuf("gscale%d" % h, [P, 256], U8) for h in range(2)]
-        gg = [sbuf("gg%d" % h, [P, 256, 4], BF16) for h in range(2)]
-
-        def weave_grows(engine_copy, h):
-            src = graw[:, :, 256 * h : 256 * (h + 1)].rearrange("p j (c i) -> p c j i", i=4)
-            engine_copy(gg[h][:].rearrange("p (c i) j -> p c j i", i=4), src)
-
-        def quant_grows(h):
-            nc.vector.quantize_mx(out=gcodes[h][:].bitcast(FP8X4), scales=gscale[h][:], in_=gg[h][:].rearrange("p e j -> p (e j)"))
-
-        weave_grows(nc.vector.tensor_copy, 0)
-        weave_grows(nc.scalar.copy, 1)
-        for r in range(4):
-            nc.vector.tensor_scalar(wq[:, r, :], pexp[r][:], rs[r // 2][:, r % 2 : r % 2 + 1], small[:, P + r : P + r + 1], ALU.mult, ALU.mult)
-        quant_grows(0)
-        wg = sbuf("wg", [P, I, 4], BF16)
-        nc.vector.tensor_copy(wg[:].rearrange("p (c i) r -> p c r i", i=4), wq[:].rearrange("p r (c i) -> p c r i", i=4))
-        quant_grows(1)
+        gb = weave_grows(nc.scalar.copy, 128, 256)
+        gc = weave_grows(nc.scalar.copy, 256, 512)
+        quant_grows(ga, 0, 128)
+        wg = [sbuf("wg%d" % h, [P, P, 4], BF16) for h in range(2)]
         wcodes = sbuf("wcodes", [P, I], U32)
         wscale = sbuf("wscale", [P, I], U8)
-        nc.vector.quantize_mx(out=wcodes[:].bitcast(FP8X4), scales=wscale[:], in_=wg[:].rearrange("p i r -> p (i r)"))
 
-        gv = [sbuf("gv%d" % k, [P, I], F32) for k in range(4)]
-        for k in range(4):
-            acc = bank(k, "gvacc%d" % k)
-            cols = slice(P * (k % 2), P * (k % 2 + 1))
-            nc.tensor.matmul_mx(out=acc[:, 0:I], lhsT=gcodes[k // 2][:, cols].bitcast(FP8X4), lhsT_scale=gscale[k // 2][:, cols],
-                                rhs=wcodes[:].bitcast(FP8X4), rhs_scale=wscale[:], start=True, stop=True)
-            nc.scalar.copy(gv[k][:], acc[:, 0:I])
+        def weigh(r, h):
+            nc.vector.tensor_scalar(wg[h][:, :, r], pexp[r][:, P * h : P * (h + 1)], rs[r // 2][:, r % 2 : r % 2 + 1], small[:, P + r : P + r + 1], ALU.mult, ALU.mult)
 
-        faded = [sbuf("faded%d" % c, [P, E], F32) for c in range(8)]
-        for c in range(8):
-            fw = bank((4, 5, 4, 5, 0, 1, 0, 1)[c], "fw%d" % c)
-            for k in range(4):
-                nc.tensor.transpose(fw[:, P * k : P * (k + 1)], oraw[c // 2][:, k, P * (c % 2) : P * (c % 2 + 1)], ident[:])
-            nc.scalar.activation(faded[c][:], fw[:], ACT.Copy, scale=fcols[:, c : c + 1])
-
-        window = [sbuf("window%d" % k, [P, T], F32) for k in range(4)]
-        for k in range(4):
-            nc.vector.memset(window[k][:], 0.0)
-
-        def scatter(k):
-            nc.vector.tensor_copy(window[k][:].indirect(offsets[:]), gv[k][:])
-
-        def finish(k):
+        for r in range(4):
             for h in range(2):
-                n = 2 * k + h
-                bk = bank((6, 7, 4, 5, 2, 3, 6, 7)[n], "back%d" % n)
-                for c in range(4):
-                    nc.tensor.transpose(bk[:, P * c : P * (c + 1)], faded[4 * h + c][:, P * k : P * (k + 1)], ident[:])
-                res = sbuf("res%d" % n, [P, 512], F32)
-                nc.vector.tensor_tensor(res[:], bk[:], window[k][:, 512 * h : 512 * (h + 1)], ALU.add)
-                nc.sync.dma_start(out=out[P * k : P * (k + 1), 512 * h : 512 * (h + 1)], in_=res[:])
+                weigh(r, h)
+        for h in range(2):
+            nc.vector.quantize_mx(out=wcodes[:, P * h : P * (h + 1)].bitcast(FP8X4), scales=wscale[:, P * h : P * (h + 1)],
+                                  in_=wg[h][:].rearrange("p i r -> p (i r)"))
 
-        scatter(0)
-        scatter(1)
-        finish(0)
-        scatter(2)
-        finish(1)
-        scatter(3)
-        finish(2)
-        finish(3)
+
+        def product(k, i0, i1, b, engine_copy):
+            acc = bank(b, "gvacc%d_%d" % (k, i0))
+            nc.tensor.matmul_mx(out=acc[:, 0 : i1 - i0], lhsT=gcodes[k].bitcast(FP8X4), lhsT_scale=gscale[k],
+                                rhs=wcodes[:, i0:i1].bitcast(FP8X4), rhs_scale=wscale[:, i0:i1], start=True, stop=True)
+            gv = sbuf("gv%d_%d" % (k, i0), [P, i1 - i0], F32)
+            engine_copy(gv[:], acc[:, 0 : i1 - i0])
+            return gv
+
+        def scatter(k, gv, i0, i1):
+            nc.vector.tensor_copy(window[k % len(window)][:].indirect(offsets[:, i0 // 16 : i1 // 16]), gv[:])
+
+        quant_grows(gb, 128, 256)
+        gv0a = product(0, 0, P, 0, nc.vector.tensor_copy)
+        gv0b = product(0, P, I, 1, nc.vector.tensor_copy)
+        scatter(0, gv0a, 0, P)
+        quant_grows(gc, 256, 512, tag="gv0_0")
+        gv1 = product(1, 0, I, 2, nc.scalar.copy)
+        NG = 0
+        faded = [sbuf("faded%d" % c, [P, E if c < 4 else E - P * NG], F32, tag=("wg0", "wg1", "gg128", "pexp3", None, None, None, None)[c]) for c in range(8)]
+
+        def fade_block(c):
+            first = 0 if c < 4 else NG
+            fw = bank((4, 5, 6, 7, 1, 2, 3, 0)[c], "fw%d" % c)
+            for k in range(first, 4):
+                src = oraw[c // 2][:, k, P * (c % 2) : P * (c % 2 + 1)] if c < 4 else oright[:, k, P * (c - 4) : P * (c - 3)]
+                nc.tensor.transpose(fw[:, P * (k - first) : P * (k - first + 1)], src, ident[:])
+            nc.scalar.activation(faded[c][:], fw[:, 0 : P * (4 - first)], ACT.Copy, scale=fcols[:, c : c + 1])
+
+        for c in range(4):
+            fade_block(c)
+        gv2 = product(2, 0, I, 3, nc.scalar.copy)
+        gv3 = product(3, 0, I, 0, nc.scalar.copy)
+        for c in range(4, 8):
+            fade_block(c)
+        scatter(0, gv0b, P, I)
+        scatter(1, gv1, 0, I)
+
+        def finish(n):
+            k, h = divmod(n, 2)
+            res = sbuf("res%d" % n, [P, 512], F32)
+            part = window[k][:, 512 * h : 512 * (h + 1)]
+            if True:
+                bk = bank((4, 1, 5, 2, 6, 3, 7, 0)[n], "back%d" % n)
+                col = P * (k - NG * h)
+                for c in range(4):
+                    nc.tensor.transpose(bk[:, P * c : P * (c + 1)], faded[4 * h + c][:, col : col + P], ident[:])
+                step = 256 if n == 7 else 512
+                for t0 in range(0, 512, step):
+                    nc.vector.tensor_tensor(res[:, t0 : t0 + step], bk[:, t0 : t0 + step], part[:, t0 : t0 + step], ALU.add)
+                    nc.sync.dma_start(out=out[P * k : P * (k + 1), 512 * h + t0 : 512 * h + t0 + step], in_=res[:, t0 : t0 + step])
+
+        scatter(2, gv2, 0, I)
+        scatter(3, gv3, 0, I)
+        for n in (0, 2, 4, 6, 1, 3, 5, 7):
+            finish(n)
+        for j, src in enumerate((gv0b, gv1, gv2, gv3)):
+            clock = sbuf("clock%d" % j, [P, 1], F32)
+            nc.gpsimd.tensor_copy(clock[:], src[:, 0:1])

@@ -5,6 +5,8 @@ from concourse.masks import make_identity
 
 D, E, T, I, Q = 512, 512, 1024, 256, 512
 P = 128
+PACK = 4
+HALF = 512
 FLOPS = 2 * D * Q * I + 2 * Q * E * I
 
 F32 = mybir.dt.float32
@@ -17,7 +19,8 @@ FP8X4 = mybir.dt.float8_e4m3fn_x4
 FP4X4 = mybir.dt.float4_e2m1fn_x4
 ALU = mybir.AluOpType
 ACT = mybir.ActivationFunctionType
-AX = mybir.AxisListType
+
+POOL_TILES = 2
 
 
 def tile_attend_bunitweights_v_kernel(tc, query, keys_words, keys_scales, qs, grows, old, fade, offs, out):
@@ -26,197 +29,205 @@ def tile_attend_bunitweights_v_kernel(tc, query, keys_words, keys_scales, qs, gr
         sb = ctx.enter_context(tc.tile_pool(name="sb", bufs=1))
         ps = ctx.enter_context(tc.psum_pool(name="ps", bufs=1))
 
-        def sbuf(name, shape, dtype, tag=None):
-            return sb.tile(shape, dtype, name=name, tag=tag or name, align_bytes=64)
+        def sbuf(name, shape, dtype, slot=None):
+            return sb.tile(shape, dtype, name=name, tag=slot or name, align_bytes=64)
 
         def bank(b, name):
-            return ps.tile([P, 512], F32, name=name, tag="bank%d" % b)
+            return ps.tile([P, HALF], F32, name=name, tag="bank%d" % b)
 
         offsets = sb.tile([P, I // 16], U16, name="offsets")
-        kwords = sbuf("kwords", [P, T], U16)
-        kscales = sbuf("kscales", [P, T], U8)
-        nc.vector.memset(kscales[:].bitcast(I32), 0)
-        nc.sync.dma_start(out=kwords[:].bitcast(I32), in_=keys_words[0].bitcast(I32))
+        key_words = sbuf("key_words", [P, T], U16)
+        key_scales = sbuf("key_scales", [P, T], U8)
+        nc.vector.memset(key_scales[:].bitcast(I32), 0)
+        nc.sync.dma_start(out=key_words[:].bitcast(I32), in_=keys_words[0].bitcast(I32))
         nc.sync.dma_start(offsets[:], offs)
         for g in range(4):
-            nc.sync.dma_start(out=kscales[32 * g : 32 * g + 4, :].bitcast(I32), in_=keys_scales[0, 4 * g : 4 * g + 4, :].bitcast(I32))
-        qv = query.rearrange("(p j) q -> p j q", j=4)
-        qraw = [sbuf("qraw%d" % h, [P, 4, 256], F32) for h in range(2)]
+            nc.sync.dma_start(out=key_scales[32 * g : 32 * g + 4, :].bitcast(I32), in_=keys_scales[0, 4 * g : 4 * g + 4, :].bitcast(I32))
+        query_view = query.rearrange("(p j) q -> p j q", j=PACK)
+        query_raw = [sbuf("query_raw%d" % h, [P, PACK, Q // 2], F32) for h in range(2)]
         for h in range(2):
-            nc.sync.dma_start(out=qraw[h][:], in_=qv[:, :, 256 * h : 256 * (h + 1)])
+            nc.sync.dma_start(out=query_raw[h][:], in_=query_view[:, :, Q // 2 * h : Q // 2 * (h + 1)])
+
         warm = sbuf("warm", [P, 1], F32)
-        half = sbuf("half", [P, 2], F32)
-        nc.vector.memset(half[:], -0.5)
-        nc.scalar.activation(warm[:], half[:, 0:1], ACT.Exp)
-        small = sbuf("small", [P, P + 4], F32)
+        minus_half = sbuf("minus_half", [P, 2], F32)
+        nc.vector.memset(minus_half[:], -0.5)
+        nc.scalar.activation(warm[:], minus_half[:, 0:1], ACT.Exp)
+        small = sbuf("small", [P, P + PACK], F32)
         nc.vector.memset(small[:], 0.0)
-        window = [sbuf("window%d" % k, [P, T], F32) for k in range(3)]
-        for w in window:
-            nc.vector.memset(w[:], 0.0)
-        nc.sync.dma_start(out=small[:, P : P + 4], in_=qs.rearrange("(p r) o -> p (r o)", r=4))
-        nc.sync.dma_start(out=small[0:8, 0:P], in_=fade.rearrange("o (c p) -> (o c) p", p=P))
+        window = [sbuf("window%d" % k, [P, T], F32) for k in range(2)]
+        for zeroed in window:
+            nc.vector.memset(zeroed[:], 0.0)
+        window.append(sbuf("window2", [P, T], F32, slot="warm"))
+        nc.gpsimd.memset(window[2][:], 0.0)
+        nc.sync.dma_start(out=small[:, P : P + PACK], in_=qs.rearrange("(p r) o -> p (r o)", r=PACK))
+        nc.sync.dma_start(out=small[0 : T // P, 0:P], in_=fade.rearrange("o (c p) -> (o c) p", p=P))
 
-        kw = sbuf("kw", [P, I], U16)
-        ks = sbuf("ks", [P, I], U8)
-        nc.vector.tensor_copy(kw[:], kwords[:].indirect(offsets[:]))
-        nc.vector.tensor_copy(ks[:], kscales[:].indirect(offsets[:]))
+        listed_words = sbuf("listed_words", [P, I], U16)
+        listed_scales = sbuf("listed_scales", [P, I], U8)
+        nc.vector.tensor_copy(listed_words[:], key_words[:].indirect(offsets[:]))
+        nc.vector.tensor_copy(listed_scales[:], key_scales[:].indirect(offsets[:]))
 
-        graw = sbuf("graw", [P, 4, E], F32, tag="kwords")
-        nc.sync.dma_start(out=graw[:], in_=grows.rearrange("(p j) e -> p j e", j=4))
+        grows_raw = sbuf("grows_raw", [P, PACK, E], F32, slot="key_words")
+        nc.sync.dma_start(out=grows_raw[:], in_=grows.rearrange("(p j) e -> p j e", j=PACK))
 
-        for j, src in enumerate((window[0], qraw[0][:, 0, :])):
-            early = sbuf("early%d" % j, [P, 1], F32)
-            nc.gpsimd.tensor_copy(early[:], src[:, 0:1])
-        qcodes = [sbuf("qcodes%d" % r, [P, P], U32) for r in range(4)]
-        qscale = [sbuf("qscale%d" % r, [P, P], U8) for r in range(4)]
+        query_codes = [sbuf("query_codes%d" % r, [P, P], U32) for r in range(PACK)]
+        query_scales = [sbuf("query_scales%d" % r, [P, P], U8) for r in range(PACK)]
+        for h in range(2):
+            dealt = query_raw[h][:].rearrange("p j (m r) -> p m j r", r=PACK)
+            woven = [sbuf("query_woven%d_%d" % (h, pair), [P, 2, P // 2, PACK], BF16) for pair in range(2)]
+            for pair, copy in enumerate((nc.vector.tensor_copy, nc.scalar.copy)):
+                copy(woven[pair][:].rearrange("p r m j -> p m j r"), dealt[:, :, :, 2 * pair : 2 * pair + 2])
+            cols = slice(P // 2 * h, P // 2 * (h + 1))
+            for r in range(PACK):
+                nc.vector.quantize_mx(
+                    out=query_codes[r][:, cols].bitcast(FP8X4),
+                    scales=query_scales[r][:, cols],
+                    in_=woven[r // 2][:, r % 2, :, :].rearrange("p m j -> p (m j)"),
+                )
 
-        def weave_query(engine_copy, h, r0, r1):
-            g = sbuf("qg%d_%d" % (h, r0), [P, r1 - r0, 64, 4], BF16)
-            src = qraw[h][:].rearrange("p j (m r) -> p m j r", r=4)[:, :, :, r0:r1]
-            engine_copy(g[:].rearrange("p r m j -> p m j r"), src)
-            return g
-
-        def quant_query(g, h, r0, r1):
-            for r in range(r0, r1):
-                nc.vector.quantize_mx(out=qcodes[r][:, 64 * h : 64 * (h + 1)].bitcast(FP8X4), scales=qscale[r][:, 64 * h : 64 * (h + 1)],
-                                      in_=g[:, r - r0, :, :].rearrange("p m j -> p (m j)"))
-
-        g0 = weave_query(nc.vector.tensor_copy, 0, 0, 4)
-        quant_query(g0, 0, 0, 4)
-        g1a = weave_query(nc.vector.tensor_copy, 1, 0, 2)
-        g1b = weave_query(nc.scalar.copy, 1, 2, 4)
-        quant_query(g1a, 1, 0, 2)
-        quant_query(g1b, 1, 2, 4)
-
-        ident = sbuf("ident", [P, P], F32, tag="qg1_0")
+        ident = sbuf("ident", [P, P], F32, slot="query_woven1_0")
         make_identity(nc, ident[:])
-        window.append(sbuf("window3", [P, T], F32, tag="qg1_2"))
+        window.append(sbuf("window3", [P, T], F32, slot="query_woven1_1"))
         nc.gpsimd.memset(window[3][:], 0.0)
 
-        ov = old.rearrange("(k p) t -> p k t", p=P)
-        oraw = [sbuf("oraw%d" % u, [P, 4, 256], F32, tag=("qraw0", "qg0_0")[u]) for u in range(2)]
+        old_view = old.rearrange("(k p) t -> p k t", p=P)
+        old_left = [sbuf("old_left%d" % u, [P, PACK, HALF // 2], F32, slot=("query_raw0", "query_woven0_1")[u]) for u in range(2)]
         for u in range(2):
-            nc.sync.dma_start(out=oraw[u][:], in_=ov[:, :, 256 * u : 256 * (u + 1)])
-        oright = sbuf("oright", [P, 4, 512], F32, tag="qraw1")
-        nc.sync.dma_start(out=oright[:], in_=ov[:, :, 512:1024])
+            nc.sync.dma_start(out=old_left[u][:], in_=old_view[:, :, HALF // 2 * u : HALF // 2 * (u + 1)])
+        old_right = sbuf("old_right", [P, PACK, HALF], F32, slot="query_raw1")
+        nc.sync.dma_start(out=old_right[:], in_=old_view[:, :, HALF:T])
 
-        scores = [bank(r, "scores%d" % r) for r in range(4)]
-        for r in range(4):
-            nc.tensor.matmul_mx(out=scores[r][:, 0:I], lhsT=qcodes[r][:].bitcast(FP8X4), lhsT_scale=qscale[r][:],
-                                rhs=kw[:].bitcast(FP4X4), rhs_scale=ks[:], start=True, stop=True)
-        neg2 = [sbuf("neg2_%d" % r, [P, I], F32) for r in range(4)]
-        neg2max = sbuf("neg2max", [P, 4], F32)
-        negmax = sbuf("negmax", [P, 4], F32)
-        pexp = [sbuf("pexp%d" % r, [P, I], F32) for r in range(4)]
-        psq = [sbuf("psq%d" % r, [P, I], F32) for r in range(4)]
-        ssum = [sbuf("ssum%d" % h, [P, 2], F32) for h in range(2)]
-        rs = [sbuf("rs%d" % h, [P, 2], F32) for h in range(2)]
-        for r in range(4):
-            nc.vector.tensor_scalar(neg2[r][:], scores[r][:, 0:I], -2.0, None, ALU.mult, ALU.min, accum_out=neg2max[:, r : r + 1])
-        for r in range(4):
-            nc.scalar.activation(psq[r][:], neg2[r][:], ACT.Exp, bias=neg2max[:, r : r + 1], scale=-1.0, accum_out=ssum[r // 2][:, r % 2 : r % 2 + 1])
+        scores = [bank(r, "scores%d" % r) for r in range(PACK)]
+        for r in range(PACK):
+            nc.tensor.matmul_mx(
+                out=scores[r][:, 0:I],
+                lhsT=query_codes[r][:].bitcast(FP8X4),
+                lhsT_scale=query_scales[r][:],
+                rhs=listed_words[:].bitcast(FP4X4),
+                rhs_scale=listed_scales[:],
+                start=True,
+                stop=True,
+            )
+        minus_2a = [sbuf("minus_2a%d" % r, [P, I], F32) for r in range(PACK)]
+        minus_2max = sbuf("minus_2max", [P, PACK], F32)
+        minus_max = sbuf("minus_max", [P, PACK], F32)
+        p_squared = [sbuf("p_squared%d" % r, [P, I], F32) for r in range(PACK)]
+        sum_squares = [sbuf("sum_squares%d" % pair, [P, 2], F32) for pair in range(2)]
+        inv_norm = sbuf("inv_norm", [P, PACK], F32)
+        for r in range(PACK):
+            nc.vector.tensor_scalar(minus_2a[r][:], scores[r][:, 0:I], -2.0, None, ALU.mult, ALU.min, accum_out=minus_2max[:, r : r + 1])
+        for r in range(PACK):
+            nc.scalar.activation(
+                p_squared[r][:], minus_2a[r][:], ACT.Exp, bias=minus_2max[:, r : r + 1], scale=-1.0,
+                accum_out=sum_squares[r // 2][:, r % 2 : r % 2 + 1],
+            )
             if r % 2:
-                nc.gpsimd.tensor_tensor(rs[r // 2][:], ssum[r // 2][:], half[:], ALU.pow)
-        gcodes = {}
-        gscale = {}
+                nc.gpsimd.tensor_tensor(inv_norm[:, r - 1 : r + 1], sum_squares[r // 2][:], minus_half[:], ALU.pow)
 
-        def weave_grows(engine_copy, e0, e1):
-            g = sbuf("gg%d" % e0, [P, e1 - e0, 4], BF16)
-            src = graw[:, :, e0:e1].rearrange("p j (c i) -> p c j i", i=4)
-            engine_copy(g[:].rearrange("p (c i) j -> p c j i", i=4), src)
-            return g
+        grows_codes = {}
+        grows_scales = {}
 
-        def quant_grows(g, e0, e1, tag=None):
-            codes = sbuf("gcodes%d" % e0, [P, e1 - e0], U32, tag=tag)
-            scale = sbuf("gscale%d" % e0, [P, e1 - e0], U8)
-            nc.vector.quantize_mx(out=codes[:].bitcast(FP8X4), scales=scale[:], in_=g[:].rearrange("p e j -> p (e j)"))
+        def weave_grows(copy, e0, e1):
+            woven_cols = sbuf("grows_woven%d" % e0, [P, e1 - e0, PACK], BF16)
+            copy(woven_cols[:].rearrange("p (c i) j -> p c j i", i=4), grows_raw[:, :, e0:e1].rearrange("p j (c i) -> p c j i", i=4))
+            return woven_cols
+
+        def quantise_grows(woven_cols, e0, e1):
+            codes = sbuf("grows_codes%d" % e0, [P, e1 - e0], U32)
+            scales = sbuf("grows_scales%d" % e0, [P, e1 - e0], U8)
+            nc.vector.quantize_mx(out=codes[:].bitcast(FP8X4), scales=scales[:], in_=woven_cols[:].rearrange("p e j -> p (e j)"))
             for e in range(e0, e1, P):
-                gcodes[e // P] = codes[:, e - e0 : e - e0 + P]
-                gscale[e // P] = scale[:, e - e0 : e - e0 + P]
+                grows_codes[e // P] = codes[:, e - e0 : e - e0 + P]
+                grows_scales[e // P] = scales[:, e - e0 : e - e0 + P]
 
-        ga = weave_grows(nc.vector.tensor_copy, 0, 128)
-        nc.vector.tensor_scalar(negmax[:], neg2max[:], 0.5, None, ALU.mult)
-        for r in range(4):
-            nc.scalar.activation(pexp[r][:], neg2[r][:], ACT.Exp, bias=negmax[:, r : r + 1], scale=-0.5)
+        woven_first = weave_grows(nc.vector.tensor_copy, 0, P)
+        nc.vector.tensor_scalar(minus_max[:], minus_2max[:], 0.5, None, ALU.mult)
+        p_exp = sbuf("p_exp", [P, PACK, I], F32)
+        for r in range(PACK):
+            nc.scalar.activation(p_exp[:, r, :], minus_2a[r][:], ACT.Exp, bias=minus_max[:, r : r + 1], scale=-0.5)
 
-        fcols = sbuf("fcols", [P, 8], F32)
-        fb = bank(3, "fbank")
-        nc.tensor.transpose(fb[:, 0:P], small[:, 0:P], ident[:])
-        nc.scalar.copy(fcols[:], fb[:, 0:8])
+        fade_cols = sbuf("fade_cols", [P, T // P], F32)
+        fade_turned = bank(3, "fade_turned")
+        nc.tensor.transpose(fade_turned[:, 0:P], small[:, 0:P], ident[:])
+        nc.scalar.copy(fade_cols[:], fade_turned[:, 0 : T // P])
 
-        gb = weave_grows(nc.scalar.copy, 128, 256)
-        gc = weave_grows(nc.scalar.copy, 256, 512)
-        quant_grows(ga, 0, 128)
-        wg = [sbuf("wg%d" % h, [P, P, 4], BF16) for h in range(2)]
-        wcodes = sbuf("wcodes", [P, I], U32)
-        wscale = sbuf("wscale", [P, I], U8)
+        woven_second = weave_grows(nc.scalar.copy, P, 2 * P)
+        woven_rest = weave_grows(nc.scalar.copy, 2 * P, E)
+        fade_spread = bank(3, "fade_spread")
+        for c in range(PACK):
+            nc.tensor.transpose(fade_spread[:, P * c : P * (c + 1)], fade_cols[:, PACK + c : PACK + c + 1].to_broadcast([P, P]), ident[:])
+        fade_right = sbuf("fade_right", [P, HALF], F32)
+        nc.scalar.copy(fade_right[:], fade_spread[:])
+        quantise_grows(woven_first, 0, P)
 
-        def weigh(r, h):
-            nc.vector.tensor_scalar(wg[h][:, :, r], pexp[r][:, P * h : P * (h + 1)], rs[r // 2][:, r % 2 : r % 2 + 1], small[:, P + r : P + r + 1], ALU.mult, ALU.mult)
+        row_factor = sbuf("row_factor", [P, PACK], F32)
+        nc.vector.tensor_tensor(row_factor[:], inv_norm[:], small[:, P : P + PACK], ALU.mult)
+        wq_woven = sbuf("wq_woven", [P, I, PACK], BF16)
+        nc.vector.tensor_tensor(
+            wq_woven[:].rearrange("p (c i) r -> p c r i", i=4),
+            p_exp[:].rearrange("p r (c i) -> p c r i", i=4),
+            row_factor[:].unsqueeze(1).unsqueeze(3).to_broadcast([P, I // 4, PACK, 4]),
+            ALU.mult,
+        )
+        wq_codes = sbuf("wq_codes", [P, I], U32)
+        wq_scales = sbuf("wq_scales", [P, I], U8)
+        nc.vector.quantize_mx(out=wq_codes[:].bitcast(FP8X4), scales=wq_scales[:], in_=wq_woven[:].rearrange("p i r -> p (i r)"))
+        quantise_grows(woven_second, P, 2 * P)
+        quantise_grows(woven_rest, 2 * P, E)
 
-        for r in range(4):
-            for h in range(2):
-                weigh(r, h)
-        for h in range(2):
-            nc.vector.quantize_mx(out=wcodes[:, P * h : P * (h + 1)].bitcast(FP8X4), scales=wscale[:, P * h : P * (h + 1)],
-                                  in_=wg[h][:].rearrange("p i r -> p (i r)"))
+        def product(k, b, copy, slot=None):
+            acc = bank(b, "gv_sums%d" % k)
+            nc.tensor.matmul_mx(
+                out=acc[:, 0:I],
+                lhsT=grows_codes[k].bitcast(FP8X4),
+                lhsT_scale=grows_scales[k],
+                rhs=wq_codes[:].bitcast(FP8X4),
+                rhs_scale=wq_scales[:],
+                start=True,
+                stop=True,
+            )
+            values = sbuf("gv%d" % k, [P, I], F32, slot=slot)
+            copy(values[:], acc[:, 0:I])
+            return values
 
+        gv = [product(0, 0, nc.vector.tensor_copy, slot="grows_woven%d" % (2 * P))]
+        for k in range(1, PACK):
+            gv.append(product(k, k, nc.scalar.copy))
 
-        def product(k, i0, i1, b, engine_copy):
-            acc = bank(b, "gvacc%d_%d" % (k, i0))
-            nc.tensor.matmul_mx(out=acc[:, 0 : i1 - i0], lhsT=gcodes[k].bitcast(FP8X4), lhsT_scale=gscale[k],
-                                rhs=wcodes[:, i0:i1].bitcast(FP8X4), rhs_scale=wscale[:, i0:i1], start=True, stop=True)
-            gv = sbuf("gv%d_%d" % (k, i0), [P, i1 - i0], F32)
-            engine_copy(gv[:], acc[:, 0 : i1 - i0])
-            return gv
+        faded_slots = ("wq_woven", "grows_woven%d" % P, "p_exp", "grows_woven0")
+        faded = []
+        for c in range(T // P):
+            left = c < PACK
+            first = 0 if left else POOL_TILES
+            turned = bank(PACK + c if left else c - PACK, "old_turned%d" % c)
+            for k in range(first, PACK):
+                if left:
+                    block = old_left[c // 2][:, k, P * (c % 2) : P * (c % 2 + 1)]
+                else:
+                    block = old_right[:, k, P * (c - PACK) : P * (c - PACK + 1)]
+                nc.tensor.transpose(turned[:, P * (k - first) : P * (k - first + 1)], block, ident[:])
+            faded.append(sbuf("faded%d" % c, [P, E - P * first], F32, slot=faded_slots[c] if left else None))
+            nc.scalar.activation(faded[c][:], turned[:, 0 : E - P * first], ACT.Copy, scale=fade_cols[:, c : c + 1])
 
-        def scatter(k, gv, i0, i1):
-            nc.vector.tensor_copy(window[k % len(window)][:].indirect(offsets[:, i0 // 16 : i1 // 16]), gv[:])
+        for k in range(PACK):
+            nc.vector.tensor_copy(window[k][:].indirect(offsets[:]), gv[k][:])
 
-        quant_grows(gb, 128, 256)
-        gv0a = product(0, 0, P, 0, nc.vector.tensor_copy)
-        gv0b = product(0, P, I, 1, nc.vector.tensor_copy)
-        scatter(0, gv0a, 0, P)
-        quant_grows(gc, 256, 512, tag="gv0_0")
-        gv1 = product(1, 0, I, 2, nc.scalar.copy)
-        NG = 0
-        faded = [sbuf("faded%d" % c, [P, E if c < 4 else E - P * NG], F32, tag=("wg0", "wg1", "gg128", "pexp3", None, None, None, None)[c]) for c in range(8)]
+        for k in range(POOL_TILES):
+            kept = sbuf("kept%d" % k, [P, HALF], F32, slot="grows_woven%d" % (2 * P))
+            nc.gpsimd.tensor_tensor(kept[:], old_right[:, k, :], fade_right[:], ALU.mult)
+            result = sbuf("result%d_1" % k, [P, HALF], F32)
+            nc.gpsimd.tensor_tensor(result[:], kept[:], window[k][:, HALF:T], ALU.add)
+            nc.scalar.dma_start(out=out[P * k : P * (k + 1), HALF:T], in_=result[:])
 
-        def fade_block(c):
-            first = 0 if c < 4 else NG
-            fw = bank((4, 5, 6, 7, 1, 2, 3, 0)[c], "fw%d" % c)
-            for k in range(first, 4):
-                src = oraw[c // 2][:, k, P * (c % 2) : P * (c % 2 + 1)] if c < 4 else oright[:, k, P * (c - 4) : P * (c - 3)]
-                nc.tensor.transpose(fw[:, P * (k - first) : P * (k - first + 1)], src, ident[:])
-            nc.scalar.activation(faded[c][:], fw[:, 0 : P * (4 - first)], ACT.Copy, scale=fcols[:, c : c + 1])
-
-        for c in range(4):
-            fade_block(c)
-        gv2 = product(2, 0, I, 3, nc.scalar.copy)
-        gv3 = product(3, 0, I, 0, nc.scalar.copy)
-        for c in range(4, 8):
-            fade_block(c)
-        scatter(0, gv0b, P, I)
-        scatter(1, gv1, 0, I)
-
-        def finish(n):
-            k, h = divmod(n, 2)
-            res = sbuf("res%d" % n, [P, 512], F32)
-            part = window[k][:, 512 * h : 512 * (h + 1)]
-            if True:
-                bk = bank((4, 1, 5, 2, 6, 3, 7, 0)[n], "back%d" % n)
-                col = P * (k - NG * h)
-                for c in range(4):
-                    nc.tensor.transpose(bk[:, P * c : P * (c + 1)], faded[4 * h + c][:, col : col + P], ident[:])
-                step = 256 if n == 7 else 512
-                for t0 in range(0, 512, step):
-                    nc.vector.tensor_tensor(res[:, t0 : t0 + step], bk[:, t0 : t0 + step], part[:, t0 : t0 + step], ALU.add)
-                    nc.sync.dma_start(out=out[P * k : P * (k + 1), 512 * h + t0 : 512 * h + t0 + step], in_=res[:, t0 : t0 + step])
-
-        scatter(2, gv2, 0, I)
-        scatter(3, gv3, 0, I)
-        for n in (0, 2, 4, 6, 1, 3, 5, 7):
-            finish(n)
-        for j, src in enumerate((gv0b, gv1, gv2, gv3)):
-            clock = sbuf("clock%d" % j, [P, 1], F32)
-            nc.gpsimd.tensor_copy(clock[:], src[:, 0:1])
+        halves = [(k, 0) for k in range(PACK)] + [(k, 1) for k in range(POOL_TILES, PACK)]
+        for k, h in halves:
+            back = bank(PACK * (1 - h) + k, "faded_back%d_%d" % (k, h))
+            col = P * (k - POOL_TILES * h)
+            for c in range(PACK):
+                nc.tensor.transpose(back[:, P * c : P * (c + 1)], faded[PACK * h + c][:, col : col + P], ident[:])
+            result = sbuf("result%d_%d" % (k, h), [P, HALF], F32)
+            step = HALF // 2 if (k, h) == halves[-1] else HALF
+            for t0 in range(0, HALF, step):
+                t = HALF * h + t0
+                nc.vector.tensor_tensor(result[:, t0 : t0 + step], back[:, t0 : t0 + step], window[k][:, t : t + step], ALU.add)
+                nc.sync.dma_start(out=out[P * k : P * (k + 1), t : t + step], in_=result[:, t0 : t0 + step])

@@ -87,8 +87,6 @@ def tile_attend_bunitweights_v_kernel(tc, query, keys_words, keys_scales, qs, gr
 
         ident = sbuf("ident", [P, P], F32, slot="query_woven1_0")
         make_identity(nc, ident[:])
-        window.append(sbuf("window3", [P, T], F32, slot="query_woven1_1"))
-        nc.gpsimd.memset(window[3][:], 0.0)
 
         old_view = old.rearrange("(k p) t -> p k t", p=P)
         old_left = [sbuf("old_left%d" % u, [P, PACK, HALF // 2], F32, slot=("query_raw0", "query_woven0_1")[u]) for u in range(2)]
@@ -153,11 +151,6 @@ def tile_attend_bunitweights_v_kernel(tc, query, keys_words, keys_scales, qs, gr
 
         woven_second = weave_grows(nc.scalar.copy, P, 2 * P)
         woven_rest = weave_grows(nc.scalar.copy, 2 * P, E)
-        fade_spread = bank(3, "fade_spread")
-        for c in range(PACK):
-            nc.tensor.transpose(fade_spread[:, P * c : P * (c + 1)], fade_cols[:, PACK + c : PACK + c + 1].to_broadcast([P, P]), ident[:])
-        fade_right = sbuf("fade_right", [P, HALF], F32)
-        nc.scalar.copy(fade_right[:], fade_spread[:])
         quantise_grows(woven_first, 0, P)
 
         row_factor = sbuf("row_factor", [P, PACK], F32)
@@ -194,7 +187,13 @@ def tile_attend_bunitweights_v_kernel(tc, query, keys_words, keys_scales, qs, gr
         for k in range(1, PACK):
             gv.append(product(k, k, nc.scalar.copy))
 
-        faded_slots = ("wq_woven", "grows_woven%d" % P, "p_exp", "grows_woven0")
+        fade_spread = bank(0, "fade_spread")
+        for c in range(PACK):
+            nc.tensor.transpose(fade_spread[:, P * c : P * (c + 1)], fade_cols[:, PACK + c : PACK + c + 1].to_broadcast([P, P]), ident[:])
+        fade_right = sbuf("fade_right", [P, HALF], F32)
+        nc.scalar.copy(fade_right[:], fade_spread[:])
+
+        faded_slots = ("wq_codes", "wq_scales", "grows_codes%d" % (2 * P), "grows_scales%d" % (2 * P))
         faded = []
         for c in range(T // P):
             left = c < PACK
@@ -209,25 +208,37 @@ def tile_attend_bunitweights_v_kernel(tc, query, keys_words, keys_scales, qs, gr
             faded.append(sbuf("faded%d" % c, [P, E - P * first], F32, slot=faded_slots[c] if left else None))
             nc.scalar.activation(faded[c][:], turned[:, 0 : E - P * first], ACT.Copy, scale=fade_cols[:, c : c + 1])
 
-        for k in range(PACK):
-            nc.vector.tensor_copy(window[k][:].indirect(offsets[:]), gv[k][:])
+        def scatter(k):
+            nc.vector.tensor_copy(window[k % len(window)][:].indirect(offsets[:]), gv[k][:])
 
-        for k in range(POOL_TILES):
+        def finish_on_gpsimd(k):
             kept = sbuf("kept%d" % k, [P, HALF], F32, slot="grows_woven%d" % (2 * P))
             nc.gpsimd.tensor_tensor(kept[:], old_right[:, k, :], fade_right[:], ALU.mult)
             result = sbuf("result%d_1" % k, [P, HALF], F32)
             nc.gpsimd.tensor_tensor(result[:], kept[:], window[k][:, HALF:T], ALU.add)
-            nc.scalar.dma_start(out=out[P * k : P * (k + 1), HALF:T], in_=result[:])
+            queue = nc.sync if k == 0 else nc.scalar
+            queue.dma_start(out=out[P * k : P * (k + 1), HALF:T], in_=result[:])
 
-        halves = [(k, 0) for k in range(PACK)] + [(k, 1) for k in range(POOL_TILES, PACK)]
-        for k, h in halves:
+        def finish_on_vector(k, h, step):
             back = bank(PACK * (1 - h) + k, "faded_back%d_%d" % (k, h))
             col = P * (k - POOL_TILES * h)
             for c in range(PACK):
                 nc.tensor.transpose(back[:, P * c : P * (c + 1)], faded[PACK * h + c][:, col : col + P], ident[:])
             result = sbuf("result%d_%d" % (k, h), [P, HALF], F32)
-            step = HALF // 2 if (k, h) == halves[-1] else HALF
             for t0 in range(0, HALF, step):
                 t = HALF * h + t0
-                nc.vector.tensor_tensor(result[:, t0 : t0 + step], back[:, t0 : t0 + step], window[k][:, t : t + step], ALU.add)
+                nc.vector.tensor_tensor(result[:, t0 : t0 + step], back[:, t0 : t0 + step], window[k % len(window)][:, t : t + step], ALU.add)
                 nc.sync.dma_start(out=out[P * k : P * (k + 1), t : t + step], in_=result[:, t0 : t0 + step])
+
+        last = PACK - 1
+        for k in range(last):
+            scatter(k)
+        for k in range(POOL_TILES):
+            finish_on_gpsimd(k)
+        for k in range(last):
+            finish_on_vector(k, 0, HALF)
+        for k in range(POOL_TILES, last):
+            finish_on_vector(k, 1, HALF)
+        scatter(last)
+        finish_on_vector(last, 0, HALF)
+        finish_on_vector(last, 1, HALF // 2)

@@ -50,31 +50,29 @@ def tile_attend_bunitweights_v_kernel(tc, query, keys_words, keys_scales, qs, gr
 
         warm = sbuf("warm", [P, 1], F32)
         minus_half = sbuf("minus_half", [P, 2], F32)
-        nc.vector.memset(minus_half[:], -0.5)
+        nc.gpsimd.memset(minus_half[:], -0.5)
         nc.scalar.activation(warm[:], minus_half[:, 0:1], ACT.Exp)
         small = sbuf("small", [P, P + PACK], F32)
         nc.vector.memset(small[:], 0.0)
         window = [sbuf("window%d" % k, [P, T], F32) for k in range(2)]
         for zeroed in window:
             nc.vector.memset(zeroed[:], 0.0)
-        window.append(sbuf("window2", [P, T], F32, slot="warm"))
-        nc.gpsimd.memset(window[2][:], 0.0)
         nc.sync.dma_start(out=small[:, P : P + PACK], in_=qs.rearrange("(p r) o -> p (r o)", r=PACK))
         nc.sync.dma_start(out=small[0 : T // P, 0:P], in_=fade.rearrange("o (c p) -> (o c) p", p=P))
 
         listed_words = sbuf("listed_words", [P, I], U16)
-        listed_scales = sbuf("listed_scales", [P, I], U8)
         nc.vector.tensor_copy(listed_words[:], key_words[:].indirect(offsets[:]))
+        listed_scales = sbuf("listed_scales", [P, I], U8, slot="key_words")
         nc.vector.tensor_copy(listed_scales[:], key_scales[:].indirect(offsets[:]))
 
-        grows_raw = sbuf("grows_raw", [P, PACK, E], F32, slot="key_words")
+        grows_raw = sbuf("grows_raw", [P, PACK, E], F32, slot="warm")
         nc.sync.dma_start(out=grows_raw[:], in_=grows.rearrange("(p j) e -> p j e", j=PACK))
 
         query_codes = [sbuf("query_codes%d" % r, [P, P], U32) for r in range(PACK)]
         query_scales = [sbuf("query_scales%d" % r, [P, P], U8) for r in range(PACK)]
         for h in range(2):
             dealt = query_raw[h][:].rearrange("p j (m r) -> p m j r", r=PACK)
-            woven = [sbuf("query_woven%d_%d" % (h, pair), [P, 2, P // 2, PACK], BF16) for pair in range(2)]
+            woven = [sbuf("query_woven%d_%d" % (h, pair), [P, 2, P // 2, PACK], BF16, slot="key_scales" if (h, pair) == (0, 0) else None) for pair in range(2)]
             for pair, copy in enumerate((nc.vector.tensor_copy, nc.scalar.copy)):
                 copy(woven[pair][:].rearrange("p r m j -> p m j r"), dealt[:, :, :, 2 * pair : 2 * pair + 2])
             cols = slice(P // 2 * h, P // 2 * (h + 1))
@@ -87,6 +85,8 @@ def tile_attend_bunitweights_v_kernel(tc, query, keys_words, keys_scales, qs, gr
 
         ident = sbuf("ident", [P, P], F32, slot="query_woven1_0")
         make_identity(nc, ident[:])
+        window.append(sbuf("window2", [P, T], F32, slot="query_woven1_1"))
+        nc.gpsimd.memset(window[2][:], 0.0)
 
         old_view = old.rearrange("(k p) t -> p k t", p=P)
         old_left = [sbuf("old_left%d" % u, [P, PACK, HALF // 2], F32, slot=("query_raw0", "query_woven0_1")[u]) for u in range(2)]

from contextlib import ExitStack

import concourse.mybir as mybir
from concourse.masks import make_identity

D, E, T, I, Q = 512, 512, 1024, 256, 512
P = 128
PACK = 4
HALF = 512
FLOPS = 2 * D * Q * I + 2 * Q * E * I

F32 = mybir.dt.float32
BF16 = mybir.dt.bfloat16
I32 = mybir.dt.int32
U32 = mybir.dt.uint32
U16 = mybir.dt.uint16
U8 = mybir.dt.uint8
FP8X4 = mybir.dt.float8_e4m3fn_x4
FP4X4 = mybir.dt.float4_e2m1fn_x4
ALU = mybir.AluOpType
ACT = mybir.ActivationFunctionType

POOL_TILES = 2


def tile_attend_bunitweights_v_kernel(tc, query, keys_words, keys_scales, qs, grows, old, fade, offs, out):
    nc = tc.nc
    with ExitStack() as ctx:
        sb = ctx.enter_context(tc.tile_pool(name="sb", bufs=1))
        ps = ctx.enter_context(tc.psum_pool(name="ps", bufs=1))

        def sbuf(name, shape, dtype, slot=None):
            return sb.tile(shape, dtype, name=name, tag=slot or name, align_bytes=64)

        def bank(b, name):
            return ps.tile([P, HALF], F32, name=name, tag="bank%d" % b)

        offsets = sb.tile([P, I // 16], U16, name="offsets")
        key_words = sbuf("key_words", [P, T], U16)
        key_scales = sbuf("key_scales", [P, T], U8)
        nc.vector.memset(key_scales[:].bitcast(I32), 0)
        nc.sync.dma_start(out=key_words[:].bitcast(I32), in_=keys_words[0].bitcast(I32))
        nc.sync.dma_start(offsets[:], offs)
        for g in range(4):
            nc.sync.dma_start(out=key_scales[32 * g : 32 * g + 4, :].bitcast(I32), in_=keys_scales[0, 4 * g : 4 * g + 4, :].bitcast(I32))
        query_view = query.rearrange("(p j) q -> p j q", j=PACK)
        query_raw = [sbuf("query_raw%d" % h, [P, PACK, Q // 2], F32) for h in range(2)]
        for h in range(2):
            nc.sync.dma_start(out=query_raw[h][:], in_=query_view[:, :, Q // 2 * h : Q // 2 * (h + 1)])

        warm = sbuf("warm", [P, 1], F32)
        minus_half = sbuf("minus_half", [P, 2], F32)
        nc.gpsimd.memset(minus_half[:], -0.5)
        nc.scalar.activation(warm[:], minus_half[:, 0:1], ACT.Exp)
        small = sbuf("small", [P, P + PACK], F32)
        nc.vector.memset(small[:], 0.0)
        window = [sbuf("window%d" % k, [P, T], F32) for k in range(2)]
        for zeroed in window:
            nc.vector.memset(zeroed[:], 0.0)
        nc.sync.dma_start(out=small[:, P : P + PACK], in_=qs.rearrange("(p r) o -> p (r o)", r=PACK))
        nc.sync.dma_start(out=small[0 : T // P, 0:P], in_=fade.rearrange("o (c p) -> (o c) p", p=P))

        listed_words = sbuf("listed_words", [P, I], U16)
        nc.vector.tensor_copy(listed_words[:], key_words[:].indirect(offsets[:]))
        listed_scales = sbuf("listed_scales", [P, I], U8, slot="key_words")
        nc.vector.tensor_copy(listed_scales[:], key_scales[:].indirect(offsets[:]))

        grows_raw = sbuf("grows_raw", [P, PACK, E], F32, slot="warm")
        nc.sync.dma_start(out=grows_raw[:], in_=grows.rearrange("(p j) e -> p j e", j=PACK))

        query_codes = [sbuf("query_codes%d" % r, [P, P], U32) for r in range(PACK)]
        query_scales = [sbuf("query_scales%d" % r, [P, P], U8) for r in range(PACK)]
        for h in range(2):
            dealt = query_raw[h][:].rearrange("p j (m r) -> p m j r", r=PACK)
            woven = [sbuf("query_woven%d_%d" % (h, pair), [P, 2, P // 2, PACK], BF16, slot="key_scales" if (h, pair) == (0, 0) else None) for pair in range(2)]
            for pair, copy in enumerate((nc.vector.tensor_copy, nc.scalar.copy)):
                copy(woven[pair][:].rearrange("p r m j -> p m j r"), dealt[:, :, :, 2 * pair : 2 * pair + 2])
            cols = slice(P // 2 * h, P // 2 * (h + 1))
            for r in range(PACK):
                nc.vector.quantize_mx(
                    out=query_codes[r][:, cols].bitcast(FP8X4),
                    scales=query_scales[r][:, cols],
                    in_=woven[r // 2][:, r % 2, :, :].rearrange("p m j -> p (m j)"),
                )

        ident = sbuf("ident", [P, P], F32, slot="query_woven1_0")
        make_identity(nc, ident[:])
        window.append(sbuf("window2", [P, T], F32, slot="query_woven1_1"))
        nc.gpsimd.memset(window[2][:], 0.0)

        old_view = old.rearrange("(k p) t -> p k t", p=P)
        old_left = [sbuf("old_left%d" % u, [P, PACK, HALF // 2], F32, slot=("query_raw0", "query_woven0_1")[u]) for u in range(2)]
        for u in range(2):
            nc.sync.dma_start(out=old_left[u][:], in_=old_view[:, :, HALF // 2 * u : HALF // 2 * (u + 1)])
        old_right = sbuf("old_right", [P, PACK, HALF], F32, slot="query_raw1")
        nc.sync.dma_start(out=old_right[:], in_=old_view[:, :, HALF:T])

        scores = [bank(r, "scores%d" % r) for r in range(PACK)]
        for r in range(PACK):
            nc.tensor.matmul_mx(
                out=scores[r][:, 0:I],
                lhsT=query_codes[r][:].bitcast(FP8X4),
                lhsT_scale=query_scales[r][:],
                rhs=listed_words[:].bitcast(FP4X4),
                rhs_scale=listed_scales[:],
                start=True,
                stop=True,
            )
        minus_2a = [sbuf("minus_2a%d" % r, [P, I], F32) for r in range(PACK)]
        minus_2max = sbuf("minus_2max", [P, PACK], F32)
        minus_max = sbuf("minus_max", [P, PACK], F32)
        p_squared = [sbuf("p_squared%d" % r, [P, I], F32) for r in range(PACK)]
        sum_squares = [sbuf("sum_squares%d" % pair, [P, 2], F32) for pair in range(2)]
        inv_norm = sbuf("inv_norm", [P, PACK], F32)
        for r in range(PACK):
            nc.vector.tensor_scalar(minus_2a[r][:], scores[r][:, 0:I], -2.0, None, ALU.mult, ALU.min, accum_out=minus_2max[:, r : r + 1])
        for r in range(PACK):
            nc.scalar.activation(
                p_squared[r][:], minus_2a[r][:], ACT.Exp, bias=minus_2max[:, r : r + 1], scale=-1.0,
                accum_out=sum_squares[r // 2][:, r % 2 : r % 2 + 1],
            )
            if r % 2:
                nc.gpsimd.tensor_tensor(inv_norm[:, r - 1 : r + 1], sum_squares[r // 2][:], minus_half[:], ALU.pow)

        grows_codes = {}
        grows_scales = {}

        def weave_grows(copy, e0, e1):
            woven_cols = sbuf("grows_woven%d" % e0, [P, e1 - e0, PACK], BF16)
            copy(woven_cols[:].rearrange("p (c i) j -> p c j i", i=4), grows_raw[:, :, e0:e1].rearrange("p j (c i) -> p c j i", i=4))
            return woven_cols

        def quantise_grows(woven_cols, e0, e1):
            codes = sbuf("grows_codes%d" % e0, [P, e1 - e0], U32)
            scales = sbuf("grows_scales%d" % e0, [P, e1 - e0], U8)
            nc.vector.quantize_mx(out=codes[:].bitcast(FP8X4), scales=scales[:], in_=woven_cols[:].rearrange("p e j -> p (e j)"))
            for e in range(e0, e1, P):
                grows_codes[e // P] = codes[:, e - e0 : e - e0 + P]
                grows_scales[e // P] = scales[:, e - e0 : e - e0 + P]

        woven_first = weave_grows(nc.vector.tensor_copy, 0, P)
        nc.vector.tensor_scalar(minus_max[:], minus_2max[:], 0.5, None, ALU.mult)
        p_exp = sbuf("p_exp", [P, PACK, I], F32)
        for r in range(PACK):
            nc.scalar.activation(p_exp[:, r, :], minus_2a[r][:], ACT.Exp, bias=minus_max[:, r : r + 1], scale=-0.5)

        fade_cols = sbuf("fade_cols", [P, T // P], F32)
        fade_turned = bank(3, "fade_turned")
        nc.tensor.transpose(fade_turned[:, 0:P], small[:, 0:P], ident[:])
        nc.scalar.copy(fade_cols[:], fade_turned[:, 0 : T // P])

        woven_second = weave_grows(nc.scalar.copy, P, 2 * P)
        woven_rest = weave_grows(nc.scalar.copy, 2 * P, E)
        quantise_grows(woven_first, 0, P)

        row_factor = sbuf("row_factor", [P, PACK], F32)
        nc.vector.tensor_tensor(row_factor[:], inv_norm[:], small[:, P : P + PACK], ALU.mult)
        wq_woven = sbuf("wq_woven", [P, I, PACK], BF16)
        nc.vector.tensor_tensor(
            wq_woven[:].rearrange("p (c i) r -> p c r i", i=4),
            p_exp[:].rearrange("p r (c i) -> p c r i", i=4),
            row_factor[:].unsqueeze(1).unsqueeze(3).to_broadcast([P, I // 4, PACK, 4]),
            ALU.mult,
        )
        wq_codes = sbuf("wq_codes", [P, I], U32)
        wq_scales = sbuf("wq_scales", [P, I], U8)
        nc.vector.quantize_mx(out=wq_codes[:].bitcast(FP8X4), scales=wq_scales[:], in_=wq_woven[:].rearrange("p i r -> p (i r)"))
        quantise_grows(woven_second, P, 2 * P)
        quantise_grows(woven_rest, 2 * P, E)

        def product(k, b, copy, slot=None):
            acc = bank(b, "gv_sums%d" % k)
            nc.tensor.matmul_mx(
                out=acc[:, 0:I],
                lhsT=grows_codes[k].bitcast(FP8X4),
                lhsT_scale=grows_scales[k],
                rhs=wq_codes[:].bitcast(FP8X4),
                rhs_scale=wq_scales[:],
                start=True,
                stop=True,
            )
            values = sbuf("gv%d" % k, [P, I], F32, slot=slot)
            copy(values[:], acc[:, 0:I])
            return values

        gv = [product(0, 0, nc.vector.tensor_copy, slot="grows_woven%d" % (2 * P))]
        for k in range(1, PACK):
            gv.append(product(k, k, nc.scalar.copy))

        fade_spread = bank(0, "fade_spread")
        for c in range(PACK):
            nc.tensor.transpose(fade_spread[:, P * c : P * (c + 1)], fade_cols[:, PACK + c : PACK + c + 1].to_broadcast([P, P]), ident[:])
        fade_right = sbuf("fade_right", [P, HALF], F32)
        nc.scalar.copy(fade_right[:], fade_spread[:])

        faded_slots = ("wq_codes", "wq_scales", "grows_codes%d" % (2 * P), "grows_scales%d" % (2 * P))
        faded = []
        for c in range(T // P):
            left = c < PACK
            first = 0 if left else POOL_TILES
            turned = bank(PACK + c if left else c - PACK, "old_turned%d" % c)
            for k in range(first, PACK):
                if left:
                    block = old_left[c // 2][:, k, P * (c % 2) : P * (c % 2 + 1)]
                else:
                    block = old_right[:, k, P * (c - PACK) : P * (c - PACK + 1)]
                nc.tensor.transpose(turned[:, P * (k - first) : P * (k - first + 1)], block, ident[:])
            faded.append(sbuf("faded%d" % c, [P, E - P * first], F32, slot=faded_slots[c] if left else None))
            nc.scalar.activation(faded[c][:], turned[:, 0 : E - P * first], ACT.Copy, scale=fade_cols[:, c : c + 1])

        def scatter(k):
            nc.vector.tensor_copy(window[k % len(window)][:].indirect(offsets[:]), gv[k][:])

        def finish_on_gpsimd(k):
            kept = sbuf("kept%d" % k, [P, HALF], F32, slot="grows_woven%d" % (2 * P))
            nc.gpsimd.tensor_tensor(kept[:], old_right[:, k, :], fade_right[:], ALU.mult)
            result = sbuf("result%d_1" % k, [P, HALF], F32)
            nc.gpsimd.tensor_tensor(result[:], kept[:], window[k][:, HALF:T], ALU.add)
            queue = nc.sync if k == 0 else nc.scalar
            queue.dma_start(out=out[P * k : P * (k + 1), HALF:T], in_=result[:])

        def finish_on_vector(k, h, step):
            back = bank(PACK * (1 - h) + k, "faded_back%d_%d" % (k, h))
            col = P * (k - POOL_TILES * h)
            for c in range(PACK):
                nc.tensor.transpose(back[:, P * c : P * (c + 1)], faded[PACK * h + c][:, col : col + P], ident[:])
            result = sbuf("result%d_%d" % (k, h), [P, HALF], F32)
            for t0 in range(0, HALF, step):
                t = HALF * h + t0
                nc.vector.tensor_tensor(result[:, t0 : t0 + step], back[:, t0 : t0 + step], window[k % len(window)][:, t : t + step], ALU.add)
                nc.sync.dma_start(out=out[P * k : P * (k + 1), t : t + step], in_=result[:, t0 : t0 + step])

        last = PACK - 1
        for k in range(last):
            scatter(k)
        for k in range(POOL_TILES):
            finish_on_gpsimd(k)
        for k in range(last):
            finish_on_vector(k, 0, HALF)
        for k in range(POOL_TILES, last):
            finish_on_vector(k, 1, HALF)
        scatter(last)
        finish_on_vector(last, 0, HALF)
        finish_on_vector(last, 1, HALF // 2)
